import numpy as np
import ml_dtypes


def mxq(x, axis, fmt="e4m3"):
    dtype, down = {"e4m3": (ml_dtypes.float8_e4m3fn, 7), "e5m2": (ml_dtypes.float8_e5m2, 14)}[fmt]
    v = np.moveaxis(np.asarray(x, np.float32).astype(ml_dtypes.bfloat16).astype(np.float64), axis, -1)
    blocks = v.reshape(v.shape[:-1] + (-1, 32))
    amax = np.abs(blocks).max(-1, keepdims=True)
    byte = np.maximum(np.where(amax > 0, np.frexp(amax)[1] - 1 + 127, 0) - down, 1)
    scale = np.exp2(byte - 127.0)
    codes = (blocks / scale).astype(np.float32).astype(dtype).astype(np.float64)
    return np.moveaxis((codes * scale).reshape(v.shape), -1, axis)


WIDE = False


def mx_kscale(k):
    if not WIDE:
        return np.ones(k)
    levels = np.array([10, -10, 5, -5, 0])
    if k % 512:
        return np.exp2(np.random.permutation(np.resize(levels, k // 32))).repeat(32)
    a = np.empty((k // 512, 16))
    for p in range(k // 512):
        a[p, :8] = np.random.permutation(np.resize(levels, 8))
        for g in range(8):
            far = levels[np.abs(levels - a[p, g]) >= 10]
            a[p, g + 8] = far[np.random.randint(len(far))]
    return np.exp2(a.ravel()).repeat(32)


def f64(x):
    return np.asarray(x).astype(np.float64)


def striped8(idx):
    return np.asarray(idx).reshape(8, -1, 16).transpose(0, 2, 1).reshape(128, -1).astype(np.uint16)


def unstriped8(offs):
    return offs.reshape(8, 16, -1).transpose(0, 2, 1).reshape(8, -1).astype(np.int64)


def pick8(x, idx, run):
    r = np.arange(len(x))
    return x[r[:, None], idx[r % (8 * run) // run]]


E2M1 = np.array([0.0, 0.5, 1.0, 1.5, 2.0, 3.0, 4.0, 6.0, -0.0, -0.5, -1.0, -1.5, -2.0, -3.0, -4.0, -6.0])


def pack_weight(w, fmt):
    k, n = w.shape
    w = f64(np.asarray(w, np.float32).astype(ml_dtypes.bfloat16)).reshape(k // 32, 32, n)
    amax = np.abs(w).max(1)
    if fmt == "e4m3":
        byte = np.frexp(amax)[1] - 1 + 127 - 7
    else:
        mant, ex = np.frexp(amax / 6.0)
        byte = np.where(mant > 0.5, ex, ex - 1) + 127
    byte = np.clip(np.where(amax > 0, byte, 1), 1, 254)
    scaled = (w * np.exp2(127.0 - byte)[:, None, :]).reshape(k, n).astype(np.float32)
    by_word = np.ascontiguousarray(scaled.reshape(k // 512, 128, 4, n).transpose(0, 1, 3, 2))
    if fmt == "e4m3":
        words = by_word.astype(ml_dtypes.float8_e4m3fn).view(np.uint8)
    else:
        c = by_word.astype(ml_dtypes.float4_e2m1fn).view(np.uint8) & 0xF
        words = (c[..., 0::2] | (c[..., 1::2] << 4)).reshape(k // 512, 128, 2 * n)
    return np.ascontiguousarray(words), np.ascontiguousarray(byte.astype(np.uint8).reshape(k // 512, 16, n))


def unpack_weight(words, scales, fmt):
    g, _, n = scales.shape
    words = np.ascontiguousarray(words).reshape(g, 128, n, -1)
    if fmt == "e4m3":
        vals = words.view(ml_dtypes.float8_e4m3fn).astype(np.float64)
    else:
        nib = np.empty((g, 128, n, 4), np.uint8)
        nib[..., 0::2] = words & 0xF
        nib[..., 1::2] = words >> 4
        vals = E2M1[nib]
    vals = vals * np.repeat(np.exp2(scales.astype(np.float64) - 127.0), 8, axis=1)[..., None]
    return vals.transpose(0, 1, 3, 2).reshape(g * 512, n)


D, V, Q, I = 512, 2048, 128, 512


def setup_inputs():
    n = np.random.standard_normal
    idx = np.stack([np.random.permutation(V)[:I] for _ in range(8)])
    fd = mx_kscale(D)
    vocp = pack_weight(n((D, V)) / fd[:, None], "e2m1")
    return {
        "hid": (n((D, Q)) * 1.0 / np.sqrt(D) * fd[:, None]).astype(np.float32),
        "voc_words": vocp[0],
        "voc_scales": vocp[1],
        "sw": (np.random.uniform(0.5, 2.0, (1, I))).astype(np.float32),
        "dhid": (n((D, Q)) * 1.0 / np.sqrt(D) * fd[:, None]).astype(np.float32),
        "base": (0.5 * n((Q, V))).astype(np.float32),
        "offs": striped8(idx),
    }


def reference(hid, voc_words, voc_scales, sw, dhid, base, offs):
    idx = unstriped8(offs)
    vocu = unpack_weight(voc_words, voc_scales, "e2m1")
    hidq = mxq(f64(hid), 0, "e4m3")
    a = hidq.T @ vocu
    dhidq = mxq(f64(dhid), 0, "e4m3")
    ta = dhidq.T @ vocu
    m1 = np.max(a, axis=1, keepdims=True)
    px = np.exp(pick8(a, idx, 16) - m1)
    zl = np.sum(px, axis=1, keepdims=True)
    dzl = np.sum(f64(sw) / (px / zl + 0.001) * px / np.square(zl) * (-1.0), axis=1, keepdims=True)
    dpx = f64(sw) / (px / zl + 0.001) / zl + dzl
    xpx = pick8(ta, idx, 16) * px
    xzl = np.sum(xpx, axis=1, keepdims=True)
    xdzl = np.sum(((xpx - xzl * px / zl) / zl * f64(sw) / np.square(px / zl + 0.001) * (-1.0) * px + xpx * f64(sw) / (px / zl + 0.001) - xzl * zl * 2.0 * f64(sw) / (px / zl + 0.001) * px / np.square(zl)) / np.square(zl) * (-1.0), axis=1, keepdims=True)
    xdpx = ((xpx - xzl * px / zl) / zl * f64(sw) / np.square(px / zl + 0.001) * (-1.0) - xzl * f64(sw) / (px / zl + 0.001) / zl) / zl + xdzl
    xe1 = xdpx * px + xpx * dpx
    xs1 = np.zeros((Q, V))
    xs1[np.arange(Q)[:, None], idx[np.arange(Q) % 128 // 16]] = xe1
    y = xs1 + f64(base)
    return y

@@ -1,0 +1,189 @@
+import math
+from contextlib import ExitStack
+
+import concourse.mybir as mybir
+
+D, V, Q, I = 512, 2048, 128, 512
+FLOPS = 2 * 2 * D * V * Q
+
+F32 = mybir.dt.float32
+BF16 = mybir.dt.bfloat16
+I32 = mybir.dt.int32
+U32 = mybir.dt.uint32
+U16 = mybir.dt.uint16
+U8 = mybir.dt.uint8
+FP8X4 = mybir.dt.float8_e4m3fn_x4
+FP4X4 = mybir.dt.float4_e2m1fn_x4
+ALU = mybir.AluOpType
+ACT = mybir.ActivationFunctionType
+
+P = 128
+PACK = 4
+N = 512
+BANKS = V // N
+EPS = 0.001
+LN2 = math.log(2.0)
+BIT_SLOPE = LN2 / 2**23
+BIT_OFFSET = 88.0
+DEGREE = 16
+STORE_WIDTHS = (256, 512, 512, 512, 256)
+
+
+def tile_attend_hvlistshare_heads_kernel(tc, hid, voc_words, voc_scales, sw, dhid, base, offs, out):
+    nc = tc.nc
+    with ExitStack() as ctx:
+        sb = ctx.enter_context(tc.tile_pool(name="sb", bufs=1))
+        ps = ctx.enter_context(tc.psum_pool(name="ps", bufs=1))
+
+        def col(name):
+            return sb.tile([P, 1], F32, name=name)
+
+        def listed(name):
+            return sb.tile([P, I], F32, name=name)
+
+        offsets = sb.tile([P, I // 16], U16, name="offsets")
+        voc_plane = sb.tile([P, V], U8, name="voc_plane", align_bytes=64)
+        nc.vector.memset(voc_plane[:].bitcast(U32), 0)
+
+        scattered = sb.tile([P, V], F32, name="scattered")
+        nc.vector.memset(scattered[:], 0.0)
+        addends = sb.tile([P, DEGREE + 1], F32, name="addends")
+        for k in range(1, DEGREE + 1):
+            nc.gpsimd.memset(addends[:, DEGREE - k : DEGREE - k + 1], 0.5 * (-1) ** (k + 1) / k)
+
+        hid_raw = sb.tile([P, PACK, Q], F32, name="hid_raw")
+        nc.sync.dma_start(out=hid_raw[:], in_=hid.rearrange("(p j) q -> p j q", j=PACK))
+        dhid_raw = sb.tile([P, PACK, Q], F32, name="dhid_raw")
+        nc.sync.dma_start(out=dhid_raw[:], in_=dhid.rearrange("(p j) q -> p j q", j=PACK))
+        for quad in range(4):
+            nc.sync.dma_start(
+                out=voc_plane[32 * quad : 32 * quad + 4, :].bitcast(I32),
+                in_=voc_scales[0][4 * quad : 4 * quad + 4, :].bitcast(I32),
+            )
+        halves = []
+        for h in range(2):
+            words = sb.tile([P, V], U8, name=f"words{h}", align_bytes=64)
+            nc.sync.dma_start(out=words[:].bitcast(I32), in_=voc_words[0][:, h * V : (h + 1) * V].bitcast(I32))
+            halves.append(words)
+        nc.sync.dma_start(offsets[:], offs)
+        weight = listed("weight")
+        nc.sync.dma_start(out=weight[:], in_=sw[0].partition_broadcast(P))
+        result = sb.tile([P, V], F32, name="result")
+        nc.sync.dma_start(out=result[:], in_=base)
+
+        def quantize(name, raw, copy):
+            grouped = sb.tile([P, Q, PACK], BF16, name=name + "_grouped", align_bytes=64)
+            copy(
+                grouped[:].rearrange("p (c i) t -> p c t i", i=4),
+                raw[:].rearrange("p t (c i) -> p c t i", i=4),
+            )
+            codes = sb.tile([P, Q], U32, name=name + "_codes", align_bytes=64)
+            plane = sb.tile([P, Q], U8, name=name + "_plane", align_bytes=64)
+            nc.vector.quantize_mx(
+                out=codes[:].bitcast(FP8X4), scales=plane[:], in_=grouped[:].rearrange("p c t -> p (c t)")
+            )
+            return codes, plane
+
+        hid_q = quantize("hid", hid_raw, nc.vector.tensor_copy)
+        dhid_q = quantize("dhid", dhid_raw, nc.scalar.copy)
+
+        def score(name, operand, j):
+            codes, plane = operand
+            bank = ps.tile([P, N], F32, name=f"{name}{j}")
+            first = (j % 2) * 2 * N
+            nc.tensor.matmul_mx(
+                out=bank[:],
+                lhsT=codes[:].bitcast(FP8X4),
+                lhsT_scale=plane[:],
+                rhs=halves[j // 2][:, first : first + 2 * N].bitcast(FP4X4),
+                rhs_scale=voc_plane[:, j * N : (j + 1) * N],
+                start=True,
+                stop=True,
+            )
+            return bank
+
+        a_all = sb.tile([P, V], F32, name="a_all")
+        ta_all = sb.tile([P, V], F32, name="ta_all")
+        bank_max = sb.tile([P, BANKS], F32, name="bank_max")
+        for j in range(BANKS):
+            bank = score("a_bank", hid_q, j)
+            nc.vector.tensor_scalar(
+                a_all[:, j * N : (j + 1) * N], bank[:], 1.0, None, ALU.mult, ALU.max,
+                accum_out=bank_max[:, j : j + 1],
+            )
+        a = listed("a")
+        nc.vector.tensor_copy(a[:], a_all[:].indirect(offsets[:]))
+        neg_max = col("neg_max")
+        nc.vector.tensor_reduce(neg_max[:], bank_max[:], mybir.AxisListType.X, ALU.max, negate=True)
+        for j in range(BANKS):
+            bank = score("ta_bank", dhid_q, j)
+            copy = nc.vector.tensor_copy if j == BANKS - 1 else nc.scalar.copy
+            copy(ta_all[:, j * N : (j + 1) * N], bank[:])
+        t = listed("t")
+        nc.vector.tensor_copy(t[:], ta_all[:].indirect(offsets[:]))
+
+        w_half = listed("w_half")
+        nc.gpsimd.tensor_scalar(w_half[:], weight[:], -0.5, 0.0, ALU.mult, ALU.add)
+        w_quarter = listed("w_quarter")
+        nc.gpsimd.tensor_scalar(w_quarter[:], weight[:], -0.25, 0.0, ALU.mult, ALU.add)
+        half_max = col("half_max")
+        nc.gpsimd.tensor_scalar(
+            half_max[:], neg_max[:], -0.5, 0.5 * (math.log(EPS) - BIT_OFFSET), ALU.mult, ALU.add
+        )
+
+        px = listed("px")
+        zl = col("zl")
+        nc.scalar.activation(px[:], a[:], ACT.Exp, bias=neg_max[:], accum_out=zl[:])
+
+        bits = zl[:].bitcast(U32)
+        guess = col("guess")
+        nc.scalar.activation(guess[:], bits, ACT.Exp, scale=-BIT_SLOPE, bias=BIT_OFFSET)
+        nc.scalar.activation(
+            addends[:, DEGREE : DEGREE + 1], bits, ACT.Identity, scale=0.5 * BIT_SLOPE, bias=half_max[:]
+        )
+        factors = sb.tile([P, DEGREE + 1], F32, name="factors", tag="factors")
+        nc.scalar.activation(
+            factors[:], guess[:].to_broadcast([P, DEGREE + 1]), ACT.Identity, scale=zl[:], bias=-1.0
+        )
+        horner = sb.tile([P, DEGREE + 1], F32, name="horner")
+        inv_zl = col("inv_zl")
+        nc.vector.reciprocal(inv_zl[:], zl[:])
+        nc.vector.tensor_tensor_scan(horner[:], factors[:], addends[:], 0.0, ALU.mult, ALU.add)
+        shift = horner[:, DEGREE : DEGREE + 1]
+        th = listed("th")
+        nc.scalar.activation(th[:], a[:], ACT.Tanh, scale=-0.5, bias=shift)
+        sq = listed("sq")
+        nc.scalar.activation(sq[:], th[:], ACT.Square)
+
+        tp = sb.tile([P, I], F32, name="tp", tag="factors")
+        t_mean = col("t_mean")
+        nc.vector.scalar_tensor_tensor(tp[:], t[:], inv_zl[:], px[:], ALU.mult, ALU.mult, accum_out=t_mean[:])
+        ws = listed("ws")
+        r_sum = col("r_sum")
+        nc.vector.scalar_tensor_tensor(
+            ws[:], th[:], 1.0, w_half[:], ALU.subtract, ALU.mult, accum_out=r_sum[:]
+        )
+        wc = listed("wc")
+        nc.vector.scalar_tensor_tensor(wc[:], t[:], t_mean[:], w_quarter[:], ALU.subtract, ALU.mult)
+        g = listed("g")
+        g_sum = col("g_sum")
+        nc.vector.scalar_tensor_tensor(g[:], sq[:], 1.0, wc[:], ALU.subtract, ALU.mult, accum_out=g_sum[:])
+
+        share = listed("share")
+        nc.scalar.activation(share[:], px[:], ACT.Identity, scale=inv_zl[:])
+        neg_c = listed("neg_c")
+        nc.scalar.activation(neg_c[:], t[:], ACT.Identity, scale=-1.0, bias=t_mean[:])
+        neg_rc = listed("neg_rc")
+        nc.scalar.activation(neg_rc[:], neg_c[:], ACT.Identity, scale=r_sum[:])
+        f = listed("f")
+        nc.vector.scalar_tensor_tensor(f[:], neg_rc[:], g_sum[:], share[:], ALU.subtract, ALU.mult)
+
+        nc.vector.tensor_tensor(scattered[:].indirect(offsets[:]), g[:], f[:], ALU.add)
+
+        first = 0
+        for n, width in enumerate(STORE_WIDTHS):
+            cols = slice(first, first + width)
+            nc.vector.tensor_tensor(result[:, cols], result[:, cols], scattered[:, cols], ALU.add)
+            queue = nc.sync if n % 2 == 0 else nc.scalar
+            queue.dma_start(out=out[:, cols], in_=result[:, cols])
+            first += width

@@ -25,7 +25,13 @@ EPS = 0.001
 LN2 = math.log(2.0)
 BIT_SLOPE = LN2 / 2**23
 BIT_OFFSET = 88.0
-DEGREE = 16
+DEGREE = 10
+HALF_LOG = [
+    -0.5 * sum((-1) ** (n + 1) / n * math.factorial(n) / (math.factorial(k) * math.factorial(n - k)) * (-1) ** (n - k) for n in range(max(k, 1), DEGREE + 1))
+    for k in range(DEGREE + 1)
+]
+STEPS = 2 * DEGREE + 1
+PASS_ORDER = [("a", 0), ("a", 1), ("a", 2), ("ta", 0), ("a", 3), ("ta", 1), ("ta", 2), ("ta", 3)]
 STORE_WIDTHS = (256, 512, 512, 512, 256)
 
 
@@ -47,9 +53,11 @@ def tile_attend_hvlistshare_heads_kernel(tc, hid, voc_words, voc_scales, sw, dhi
 
         scattered = sb.tile([P, V], F32, name="scattered")
         nc.vector.memset(scattered[:], 0.0)
-        addends = sb.tile([P, DEGREE + 1], F32, name="addends")
+        addends = sb.tile([P, STEPS], F32, name="addends")
+        nc.gpsimd.memset(addends[:], 0.0)
         for k in range(1, DEGREE + 1):
-            nc.gpsimd.memset(addends[:, DEGREE - k : DEGREE - k + 1], 0.5 * (-1) ** (k + 1) / k)
+            place = addends[:, 2 * (DEGREE - k) : 2 * (DEGREE - k) + 1]
+            nc.gpsimd.tensor_scalar(place, place, 1.0, HALF_LOG[k], ALU.mult, ALU.add)
 
         hid_raw = sb.tile([P, PACK, Q], F32, name="hid_raw")
         nc.sync.dma_start(out=hid_raw[:], in_=hid.rearrange("(p j) q -> p j q", j=PACK))
@@ -105,30 +113,27 @@ def tile_attend_hvlistshare_heads_kernel(tc, hid, voc_words, voc_scales, sw, dhi
         a_all = sb.tile([P, V], F32, name="a_all")
         ta_all = sb.tile([P, V], F32, name="ta_all")
         bank_max = sb.tile([P, BANKS], F32, name="bank_max")
-        for j in range(BANKS):
-            bank = score("a_bank", hid_q, j)
-            nc.vector.tensor_scalar(
-                a_all[:, j * N : (j + 1) * N], bank[:], 1.0, None, ALU.mult, ALU.max,
-                accum_out=bank_max[:, j : j + 1],
-            )
-        a = listed("a")
-        nc.vector.tensor_copy(a[:], a_all[:].indirect(offsets[:]))
+        for name, j in PASS_ORDER:
+            cols = slice(j * N, (j + 1) * N)
+            if name == "a":
+                bank = score("a_bank", hid_q, j)
+                nc.vector.tensor_scalar(
+                    a_all[:, cols], bank[:], 1.0, None, ALU.mult, ALU.max, accum_out=bank_max[:, j : j + 1]
+                )
+            else:
+                bank = score("ta_bank", dhid_q, j)
+                nc.scalar.copy(ta_all[:, cols], bank[:])
         neg_max = col("neg_max")
         nc.vector.tensor_reduce(neg_max[:], bank_max[:], mybir.AxisListType.X, ALU.max, negate=True)
-        for j in range(BANKS):
-            bank = score("ta_bank", dhid_q, j)
-            copy = nc.vector.tensor_copy if j == BANKS - 1 else nc.scalar.copy
-            copy(ta_all[:, j * N : (j + 1) * N], bank[:])
+        a = sb.tile([P, I], F32, name="a", tag="a")
+        nc.vector.tensor_copy(a[:], a_all[:].indirect(offsets[:]))
         t = listed("t")
-        nc.vector.tensor_copy(t[:], ta_all[:].indirect(offsets[:]))
+        nc.vector.tensor_scalar(t[:], ta_all[:].indirect(offsets[:]), -0.5, 0.0, ALU.mult, ALU.add)
 
-        w_half = listed("w_half")
-        nc.gpsimd.tensor_scalar(w_half[:], weight[:], -0.5, 0.0, ALU.mult, ALU.add)
-        w_quarter = listed("w_quarter")
-        nc.gpsimd.tensor_scalar(w_quarter[:], weight[:], -0.25, 0.0, ALU.mult, ALU.add)
         half_max = col("half_max")
-        nc.gpsimd.tensor_scalar(
-            half_max[:], neg_max[:], -0.5, 0.5 * (math.log(EPS) - BIT_OFFSET), ALU.mult, ALU.add
+        nc.scalar.activation(
+            half_max[:], neg_max[:], ACT.Identity, scale=0.5,
+            bias=HALF_LOG[0] - 0.5 * (math.log(EPS) - BIT_OFFSET),
         )
 
         px = listed("px")
@@ -136,24 +141,25 @@ def tile_attend_hvlistshare_heads_kernel(tc, hid, voc_words, voc_scales, sw, dhi
         nc.scalar.activation(px[:], a[:], ACT.Exp, bias=neg_max[:], accum_out=zl[:])
 
         bits = zl[:].bitcast(U32)
-        guess = col("guess")
-        nc.scalar.activation(guess[:], bits, ACT.Exp, scale=-BIT_SLOPE, bias=BIT_OFFSET)
+        factors = sb.tile([P, STEPS], F32, name="factors", tag="factors")
         nc.scalar.activation(
-            addends[:, DEGREE : DEGREE + 1], bits, ACT.Identity, scale=0.5 * BIT_SLOPE, bias=half_max[:]
+            factors[:, 1::2], bits.to_broadcast([P, DEGREE]), ACT.Exp, scale=-BIT_SLOPE, bias=BIT_OFFSET
         )
-        factors = sb.tile([P, DEGREE + 1], F32, name="factors", tag="factors")
+        nc.scalar.activation(factors[:, 0::2], zl[:].to_broadcast([P, DEGREE + 1]), ACT.Identity)
         nc.scalar.activation(
-            factors[:], guess[:].to_broadcast([P, DEGREE + 1]), ACT.Identity, scale=zl[:], bias=-1.0
+            addends[:, STEPS - 1 : STEPS], bits, ACT.Identity, scale=-0.5 * BIT_SLOPE, bias=half_max[:]
         )
-        horner = sb.tile([P, DEGREE + 1], F32, name="horner")
+        horner = sb.tile([P, STEPS], F32, name="horner")
         inv_zl = col("inv_zl")
         nc.vector.reciprocal(inv_zl[:], zl[:])
         nc.vector.tensor_tensor_scan(horner[:], factors[:], addends[:], 0.0, ALU.mult, ALU.add)
-        shift = horner[:, DEGREE : DEGREE + 1]
+        shift = horner[:, STEPS - 1 : STEPS]
         th = listed("th")
-        nc.scalar.activation(th[:], a[:], ACT.Tanh, scale=-0.5, bias=shift)
+        nc.scalar.activation(th[:], a[:], ACT.Tanh, scale=0.5, bias=shift)
+        share = sb.tile([P, I], F32, name="share", tag="a")
+        nc.scalar.activation(share[:], px[:], ACT.Identity, scale=inv_zl[:])
         sq = listed("sq")
-        nc.scalar.activation(sq[:], th[:], ACT.Square)
+        nc.scalar.activation(sq[:], th[:], ACT.Square, scale=math.sqrt(0.5))
 
         tp = sb.tile([P, I], F32, name="tp", tag="factors")
         t_mean = col("t_mean")
@@ -161,20 +167,18 @@ def tile_attend_hvlistshare_heads_kernel(tc, hid, voc_words, voc_scales, sw, dhi
         ws = listed("ws")
         r_sum = col("r_sum")
         nc.vector.scalar_tensor_tensor(
-            ws[:], th[:], 1.0, w_half[:], ALU.subtract, ALU.mult, accum_out=r_sum[:]
+            ws[:], th[:], 1.0, weight[:], ALU.add, ALU.mult, accum_out=r_sum[:]
         )
         wc = listed("wc")
-        nc.vector.scalar_tensor_tensor(wc[:], t[:], t_mean[:], w_quarter[:], ALU.subtract, ALU.mult)
+        nc.vector.scalar_tensor_tensor(wc[:], t[:], t_mean[:], weight[:], ALU.subtract, ALU.mult)
+        r_mean = col("r_mean")
+        nc.vector.tensor_scalar(r_mean[:], r_sum[:], t_mean[:], -1.0, ALU.mult, ALU.mult)
         g = listed("g")
         g_sum = col("g_sum")
-        nc.vector.scalar_tensor_tensor(g[:], sq[:], 1.0, wc[:], ALU.subtract, ALU.mult, accum_out=g_sum[:])
+        nc.vector.scalar_tensor_tensor(g[:], sq[:], 0.5, wc[:], ALU.subtract, ALU.mult, accum_out=g_sum[:])
 
-        share = listed("share")
-        nc.scalar.activation(share[:], px[:], ACT.Identity, scale=inv_zl[:])
-        neg_c = listed("neg_c")
-        nc.scalar.activation(neg_c[:], t[:], ACT.Identity, scale=-1.0, bias=t_mean[:])
         neg_rc = listed("neg_rc")
-        nc.scalar.activation(neg_rc[:], neg_c[:], ACT.Identity, scale=r_sum[:])
+        nc.scalar.activation(neg_rc[:], t[:], ACT.Identity, scale=r_sum[:], bias=r_mean[:])
         f = listed("f")
         nc.vector.scalar_tensor_tensor(f[:], neg_rc[:], g_sum[:], share[:], ALU.subtract, ALU.mult)
 

@@ -26,9 +26,9 @@ LN2 = math.log(2.0)
 BIT_SLOPE = LN2 / 2**23
 BIT_OFFSET = 88.0
 DEGREE = 10
-HALF_LOG = [
-    -0.5 * sum((-1) ** (n + 1) / n * math.factorial(n) / (math.factorial(k) * math.factorial(n - k)) * (-1) ** (n - k) for n in range(max(k, 1), DEGREE + 1))
-    for k in range(DEGREE + 1)
+HALF_LOG = [0.5 * sum(1.0 / n for n in range(1, DEGREE + 1))] + [
+    0.5 * (-1) ** k * math.factorial(DEGREE) / (math.factorial(k) * math.factorial(DEGREE - k) * k)
+    for k in range(1, DEGREE + 1)
 ]
 STEPS = 2 * DEGREE + 1
 PASS_ORDER = [("a", 0), ("a", 1), ("a", 2), ("ta", 0), ("a", 3), ("ta", 1), ("ta", 2), ("ta", 3)]
@@ -55,9 +55,11 @@ def tile_attend_hvlistshare_heads_kernel(tc, hid, voc_words, voc_scales, sw, dhi
         nc.vector.memset(scattered[:], 0.0)
         addends = sb.tile([P, STEPS], F32, name="addends")
         nc.gpsimd.memset(addends[:], 0.0)
+        one = col("one")
+        nc.gpsimd.memset(one[:], 1.0)
         for k in range(1, DEGREE + 1):
-            place = addends[:, 2 * (DEGREE - k) : 2 * (DEGREE - k) + 1]
-            nc.gpsimd.tensor_scalar(place, place, 1.0, HALF_LOG[k], ALU.mult, ALU.add)
+            place = 2 * (DEGREE - k)
+            nc.scalar.activation(addends[:, place : place + 1], one[:], ACT.Identity, scale=HALF_LOG[k])
 
         hid_raw = sb.tile([P, PACK, Q], F32, name="hid_raw")
         nc.sync.dma_start(out=hid_raw[:], in_=hid.rearrange("(p j) q -> p j q", j=PACK))
@@ -156,29 +158,27 @@ def tile_attend_hvlistshare_heads_kernel(tc, hid, voc_words, voc_scales, sw, dhi
         shift = horner[:, STEPS - 1 : STEPS]
         th = listed("th")
         nc.scalar.activation(th[:], a[:], ACT.Tanh, scale=0.5, bias=shift)
-        share = sb.tile([P, I], F32, name="share", tag="a")
-        nc.scalar.activation(share[:], px[:], ACT.Identity, scale=inv_zl[:])
         sq = listed("sq")
         nc.scalar.activation(sq[:], th[:], ACT.Square, scale=math.sqrt(0.5))
 
+        share = sb.tile([P, I], F32, name="share", tag="a")
+        nc.scalar.activation(share[:], px[:], ACT.Identity, scale=inv_zl[:])
         tp = sb.tile([P, I], F32, name="tp", tag="factors")
         t_mean = col("t_mean")
         nc.vector.scalar_tensor_tensor(tp[:], t[:], inv_zl[:], px[:], ALU.mult, ALU.mult, accum_out=t_mean[:])
+        wc = listed("wc")
+        nc.vector.scalar_tensor_tensor(wc[:], t[:], t_mean[:], weight[:], ALU.subtract, ALU.mult)
         ws = listed("ws")
         r_sum = col("r_sum")
         nc.vector.scalar_tensor_tensor(
             ws[:], th[:], 1.0, weight[:], ALU.add, ALU.mult, accum_out=r_sum[:]
         )
-        wc = listed("wc")
-        nc.vector.scalar_tensor_tensor(wc[:], t[:], t_mean[:], weight[:], ALU.subtract, ALU.mult)
-        r_mean = col("r_mean")
-        nc.vector.tensor_scalar(r_mean[:], r_sum[:], t_mean[:], -1.0, ALU.mult, ALU.mult)
         g = listed("g")
         g_sum = col("g_sum")
         nc.vector.scalar_tensor_tensor(g[:], sq[:], 0.5, wc[:], ALU.subtract, ALU.mult, accum_out=g_sum[:])
 
         neg_rc = listed("neg_rc")
-        nc.scalar.activation(neg_rc[:], t[:], ACT.Identity, scale=r_sum[:], bias=r_mean[:])
+        nc.vector.tensor_scalar(neg_rc[:], t[:], t_mean[:], r_sum[:], ALU.subtract, ALU.mult)
         f = listed("f")
         nc.vector.scalar_tensor_tensor(f[:], neg_rc[:], g_sum[:], share[:], ALU.subtract, ALU.mult)
 

@@ -2,6 +2,7 @@ import math
 from contextlib import ExitStack
 
 import concourse.mybir as mybir
+from concourse.masks import make_identity
 
 D, V, Q, I = 512, 2048, 128, 512
 FLOPS = 2 * 2 * D * V * Q
@@ -61,14 +62,16 @@ def tile_attend_hvlistshare_heads_kernel(tc, hid, voc_words, voc_scales, sw, dhi
             place = 2 * (DEGREE - k)
             nc.scalar.activation(addends[:, place : place + 1], one[:], ACT.Identity, scale=HALF_LOG[k])
 
+        identity = sb.tile([P, P], F32, name="identity")
+        make_identity(nc, identity[:])
+
         hid_raw = sb.tile([P, PACK, Q], F32, name="hid_raw")
         nc.sync.dma_start(out=hid_raw[:], in_=hid.rearrange("(p j) q -> p j q", j=PACK))
         dhid_raw = sb.tile([P, PACK, Q], F32, name="dhid_raw")
         nc.sync.dma_start(out=dhid_raw[:], in_=dhid.rearrange("(p j) q -> p j q", j=PACK))
-        for quad in range(4):
+        for row in range(4):
             nc.sync.dma_start(
-                out=voc_plane[32 * quad : 32 * quad + 4, :].bitcast(I32),
-                in_=voc_scales[0][4 * quad : 4 * quad + 4, :].bitcast(I32),
+                out=voc_plane[row:P:32, :].bitcast(I32), in_=voc_scales[0][row::4, :].bitcast(I32)
             )
         halves = []
         for h in range(2):
@@ -76,8 +79,8 @@ def tile_attend_hvlistshare_heads_kernel(tc, hid, voc_words, voc_scales, sw, dhi
             nc.sync.dma_start(out=words[:].bitcast(I32), in_=voc_words[0][:, h * V : (h + 1) * V].bitcast(I32))
             halves.append(words)
         nc.sync.dma_start(offsets[:], offs)
-        weight = listed("weight")
-        nc.sync.dma_start(out=weight[:], in_=sw[0].partition_broadcast(P))
+        weight_cols = sb.tile([P, PACK], F32, name="weight_cols")
+        nc.sync.dma_start(out=weight_cols[:], in_=sw[0].rearrange("(p j) -> p j", j=PACK))
         result = sb.tile([P, V], F32, name="result")
         nc.sync.dma_start(out=result[:], in_=base)
 
@@ -99,7 +102,7 @@ def tile_attend_hvlistshare_heads_kernel(tc, hid, voc_words, voc_scales, sw, dhi
 
         def score(name, operand, j):
             codes, plane = operand
-            bank = ps.tile([P, N], F32, name=f"{name}{j}")
+            bank = ps.tile([P, N], F32, name=f"{name}{j}", tag=f"{name}{j}")
             first = (j % 2) * 2 * N
             nc.tensor.matmul_mx(
                 out=bank[:],
@@ -125,6 +128,14 @@ def tile_attend_hvlistshare_heads_kernel(tc, hid, voc_words, voc_scales, sw, dhi
             else:
                 bank = score("ta_bank", dhid_q, j)
                 nc.scalar.copy(ta_all[:, cols], bank[:])
+        weight_bank = ps.tile([P, PACK, P], F32, name="weight_bank", tag="a_bank3")
+        for j in range(PACK):
+            nc.tensor.transpose(weight_bank[:, j, :], weight_cols[:, j : j + 1].to_broadcast([P, P]), identity[:])
+        weight = weight_bank[:].rearrange("q j p -> q p j")
+
+        def by_word(tile):
+            return tile[:].rearrange("q (p j) -> q p j", j=PACK)
+
         neg_max = col("neg_max")
         nc.vector.tensor_reduce(neg_max[:], bank_max[:], mybir.AxisListType.X, ALU.max, negate=True)
         a = sb.tile([P, I], F32, name="a", tag="a")
@@ -167,11 +178,11 @@ def tile_attend_hvlistshare_heads_kernel(tc, hid, voc_words, voc_scales, sw, dhi
         t_mean = col("t_mean")
         nc.vector.scalar_tensor_tensor(tp[:], t[:], inv_zl[:], px[:], ALU.mult, ALU.mult, accum_out=t_mean[:])
         wc = listed("wc")
-        nc.vector.scalar_tensor_tensor(wc[:], t[:], t_mean[:], weight[:], ALU.subtract, ALU.mult)
+        nc.vector.scalar_tensor_tensor(by_word(wc), by_word(t), t_mean[:], weight, ALU.subtract, ALU.mult)
         ws = listed("ws")
         r_sum = col("r_sum")
         nc.vector.scalar_tensor_tensor(
-            ws[:], th[:], 1.0, weight[:], ALU.add, ALU.mult, accum_out=r_sum[:]
+            by_word(ws), by_word(th), 1.0, weight, ALU.add, ALU.mult, accum_out=r_sum[:]
         )
         g = listed("g")
         g_sum = col("g_sum")

import math
from contextlib import ExitStack

import concourse.mybir as mybir
from concourse.masks import make_identity

D, V, Q, I = 512, 2048, 128, 512
FLOPS = 2 * 2 * D * V * Q

F32 = mybir.dt.float32
BF16 = mybir.dt.bfloat16
I32 = mybir.dt.int32
U32 = mybir.dt.uint32
U16 = mybir.dt.uint16
U8 = mybir.dt.uint8
FP8X4 = mybir.dt.float8_e4m3fn_x4
FP4X4 = mybir.dt.float4_e2m1fn_x4
ALU = mybir.AluOpType
ACT = mybir.ActivationFunctionType

P = 128
PACK = 4
N = 512
BANKS = V // N
EPS = 0.001
LN2 = math.log(2.0)
BIT_SLOPE = LN2 / 2**23
BIT_OFFSET = 88.0
DEGREE = 10
HALF_LOG = [0.5 * sum(1.0 / n for n in range(1, DEGREE + 1))] + [
    0.5 * (-1) ** k * math.factorial(DEGREE) / (math.factorial(k) * math.factorial(DEGREE - k) * k)
    for k in range(1, DEGREE + 1)
]
STEPS = 2 * DEGREE + 1
PASS_ORDER = [("a", 0), ("a", 1), ("a", 2), ("ta", 0), ("a", 3), ("ta", 1), ("ta", 2), ("ta", 3)]
STORE_WIDTHS = (256, 512, 512, 512, 256)


def tile_attend_hvlistshare_heads_kernel(tc, hid, voc_words, voc_scales, sw, dhid, base, offs, out):
    nc = tc.nc
    with ExitStack() as ctx:
        sb = ctx.enter_context(tc.tile_pool(name="sb", bufs=1))
        ps = ctx.enter_context(tc.psum_pool(name="ps", bufs=1))

        def col(name):
            return sb.tile([P, 1], F32, name=name)

        def listed(name):
            return sb.tile([P, I], F32, name=name)

        offsets = sb.tile([P, I // 16], U16, name="offsets")
        voc_plane = sb.tile([P, V], U8, name="voc_plane", align_bytes=64)
        nc.vector.memset(voc_plane[:].bitcast(U32), 0)

        scattered = sb.tile([P, V], F32, name="scattered")
        nc.vector.memset(scattered[:], 0.0)
        addends = sb.tile([P, STEPS], F32, name="addends")
        nc.gpsimd.memset(addends[:], 0.0)
        one = col("one")
        nc.gpsimd.memset(one[:], 1.0)
        for k in range(1, DEGREE + 1):
            place = 2 * (DEGREE - k)
            nc.scalar.activation(addends[:, place : place + 1], one[:], ACT.Identity, scale=HALF_LOG[k])

        identity = sb.tile([P, P], F32, name="identity")
        make_identity(nc, identity[:])

        hid_raw = sb.tile([P, PACK, Q], F32, name="hid_raw")
        nc.sync.dma_start(out=hid_raw[:], in_=hid.rearrange("(p j) q -> p j q", j=PACK))
        dhid_raw = sb.tile([P, PACK, Q], F32, name="dhid_raw")
        nc.sync.dma_start(out=dhid_raw[:], in_=dhid.rearrange("(p j) q -> p j q", j=PACK))
        for row in range(4):
            nc.sync.dma_start(
                out=voc_plane[row:P:32, :].bitcast(I32), in_=voc_scales[0][row::4, :].bitcast(I32)
            )
        halves = []
        for h in range(2):
            words = sb.tile([P, V], U8, name=f"words{h}", align_bytes=64)
            nc.sync.dma_start(out=words[:].bitcast(I32), in_=voc_words[0][:, h * V : (h + 1) * V].bitcast(I32))
            halves.append(words)
        nc.sync.dma_start(offsets[:], offs)
        weight_cols = sb.tile([P, PACK], F32, name="weight_cols")
        nc.sync.dma_start(out=weight_cols[:], in_=sw[0].rearrange("(p j) -> p j", j=PACK))
        result = sb.tile([P, V], F32, name="result")
        nc.sync.dma_start(out=result[:], in_=base)

        def quantize(name, raw, copy):
            grouped = sb.tile([P, Q, PACK], BF16, name=name + "_grouped", align_bytes=64)
            copy(
                grouped[:].rearrange("p (c i) t -> p c t i", i=4),
                raw[:].rearrange("p t (c i) -> p c t i", i=4),
            )
            codes = sb.tile([P, Q], U32, name=name + "_codes", align_bytes=64)
            plane = sb.tile([P, Q], U8, name=name + "_plane", align_bytes=64)
            nc.vector.quantize_mx(
                out=codes[:].bitcast(FP8X4), scales=plane[:], in_=grouped[:].rearrange("p c t -> p (c t)")
            )
            return codes, plane

        hid_q = quantize("hid", hid_raw, nc.vector.tensor_copy)
        dhid_q = quantize("dhid", dhid_raw, nc.scalar.copy)

        def score(name, operand, j):
            codes, plane = operand
            bank = ps.tile([P, N], F32, name=f"{name}{j}", tag=f"{name}{j}")
            first = (j % 2) * 2 * N
            nc.tensor.matmul_mx(
                out=bank[:],
                lhsT=codes[:].bitcast(FP8X4),
                lhsT_scale=plane[:],
                rhs=halves[j // 2][:, first : first + 2 * N].bitcast(FP4X4),
                rhs_scale=voc_plane[:, j * N : (j + 1) * N],
                start=True,
                stop=True,
            )
            return bank

        a_all = sb.tile([P, V], F32, name="a_all")
        ta_all = sb.tile([P, V], F32, name="ta_all")
        bank_max = sb.tile([P, BANKS], F32, name="bank_max")
        for name, j in PASS_ORDER:
            cols = slice(j * N, (j + 1) * N)
            if name == "a":
                bank = score("a_bank", hid_q, j)
                nc.vector.tensor_scalar(
                    a_all[:, cols], bank[:], 1.0, None, ALU.mult, ALU.max, accum_out=bank_max[:, j : j + 1]
                )
            else:
                bank = score("ta_bank", dhid_q, j)
                nc.scalar.copy(ta_all[:, cols], bank[:])
        weight_bank = ps.tile([P, PACK, P], F32, name="weight_bank", tag="a_bank3")
        for j in range(PACK):
            nc.tensor.transpose(weight_bank[:, j, :], weight_cols[:, j : j + 1].to_broadcast([P, P]), identity[:])
        weight = weight_bank[:].rearrange("q j p -> q p j")

        def by_word(tile):
            return tile[:].rearrange("q (p j) -> q p j", j=PACK)

        neg_max = col("neg_max")
        nc.vector.tensor_reduce(neg_max[:], bank_max[:], mybir.AxisListType.X, ALU.max, negate=True)
        a = sb.tile([P, I], F32, name="a", tag="a")
        nc.vector.tensor_copy(a[:], a_all[:].indirect(offsets[:]))
        t = listed("t")
        nc.vector.tensor_scalar(t[:], ta_all[:].indirect(offsets[:]), -0.5, 0.0, ALU.mult, ALU.add)

        half_max = col("half_max")
        nc.scalar.activation(
            half_max[:], neg_max[:], ACT.Identity, scale=0.5,
            bias=HALF_LOG[0] - 0.5 * (math.log(EPS) - BIT_OFFSET),
        )

        px = listed("px")
        zl = col("zl")
        nc.scalar.activation(px[:], a[:], ACT.Exp, bias=neg_max[:], accum_out=zl[:])

        bits = zl[:].bitcast(U32)
        factors = sb.tile([P, STEPS], F32, name="factors", tag="factors")
        nc.scalar.activation(
            factors[:, 1::2], bits.to_broadcast([P, DEGREE]), ACT.Exp, scale=-BIT_SLOPE, bias=BIT_OFFSET
        )
        nc.scalar.activation(factors[:, 0::2], zl[:].to_broadcast([P, DEGREE + 1]), ACT.Identity)
        nc.scalar.activation(
            addends[:, STEPS - 1 : STEPS], bits, ACT.Identity, scale=-0.5 * BIT_SLOPE, bias=half_max[:]
        )
        horner = sb.tile([P, STEPS], F32, name="horner")
        inv_zl = col("inv_zl")
        nc.vector.reciprocal(inv_zl[:], zl[:])
        nc.vector.tensor_tensor_scan(horner[:], factors[:], addends[:], 0.0, ALU.mult, ALU.add)
        shift = horner[:, STEPS - 1 : STEPS]
        th = listed("th")
        nc.scalar.activation(th[:], a[:], ACT.Tanh, scale=0.5, bias=shift)
        sq = listed("sq")
        nc.scalar.activation(sq[:], th[:], ACT.Square, scale=math.sqrt(0.5))

        share = sb.tile([P, I], F32, name="share", tag="a")
        nc.scalar.activation(share[:], px[:], ACT.Identity, scale=inv_zl[:])
        tp = sb.tile([P, I], F32, name="tp", tag="factors")
        t_mean = col("t_mean")
        nc.vector.scalar_tensor_tensor(tp[:], t[:], inv_zl[:], px[:], ALU.mult, ALU.mult, accum_out=t_mean[:])
        wc = listed("wc")
        nc.vector.scalar_tensor_tensor(by_word(wc), by_word(t), t_mean[:], weight, ALU.subtract, ALU.mult)
        ws = listed("ws")
        r_sum = col("r_sum")
        nc.vector.scalar_tensor_tensor(
            by_word(ws), by_word(th), 1.0, weight, ALU.add, ALU.mult, accum_out=r_sum[:]
        )
        g = listed("g")
        g_sum = col("g_sum")
        nc.vector.scalar_tensor_tensor(g[:], sq[:], 0.5, wc[:], ALU.subtract, ALU.mult, accum_out=g_sum[:])

        neg_rc = listed("neg_rc")
        nc.vector.tensor_scalar(neg_rc[:], t[:], t_mean[:], r_sum[:], ALU.subtract, ALU.mult)
        f = listed("f")
        nc.vector.scalar_tensor_tensor(f[:], neg_rc[:], g_sum[:], share[:], ALU.subtract, ALU.mult)

        nc.vector.tensor_tensor(scattered[:].indirect(offsets[:]), g[:], f[:], ALU.add)

        first = 0
        for n, width in enumerate(STORE_WIDTHS):
            cols = slice(first, first + width)
            nc.vector.tensor_tensor(result[:, cols], result[:, cols], scattered[:, cols], ALU.add)
            queue = nc.sync if n % 2 == 0 else nc.scalar
            queue.dma_start(out=out[:, cols], in_=result[:, cols])
            first += width
